import numpy as np
import ml_dtypes

BF16 = ml_dtypes.bfloat16


def bf(x):
    return np.asarray(x, np.float32).astype(BF16)


def f32(x):
    return np.asarray(x, np.float32)


def f64(x):
    return np.asarray(x).astype(np.float64)


def striped(idx):
    return np.tile(idx.reshape(-1, 16).T, (8, 1))


def rows(idx, k):
    return np.tile(idx, (k, 1))


def look(tab, idx):
    return np.take_along_axis(f64(tab), rows(idx, len(tab)), axis=1)


K, S, V, N = 256, 2048, 2048, 2048


def silu(v):
    return v / (1.0 + np.exp(-v))


def setup_inputs():
    return {"tab": bf(np.random.standard_normal((K, S))), "y": f32(np.random.standard_normal((K, V))), "offs": striped(np.random.permutation(S)[:N])}


def reference(tab, y, offs):
    idx = offs[:16].T.reshape(-1)
    t = look(tab, idx)
    x = silu(t) * f64(y)
    return x

@@ -1,0 +1,47 @@
+import concourse.mybir as mybir
+
+BF16, F32, U16 = mybir.dt.bfloat16, mybir.dt.float32, mybir.dt.uint16
+SILU = mybir.ActivationFunctionType.Silu
+MULT = mybir.AluOpType.mult
+
+PARTITIONS = 128
+OFFSETS_PER_COLUMN = 16
+PIECE = 512
+
+
+def tile_lookup_gate_silu_out_kernel(tc, tab, y, offs, out):
+    nc = tc.nc
+    rows, columns = tab.shape
+    entries = y.shape[1]
+    blocks = rows // PARTITIONS
+    pieces = entries // PIECE
+    piece_columns = PIECE // OFFSETS_PER_COLUMN
+
+    with (
+        tc.tile_pool(name="held", bufs=1) as held,
+        tc.tile_pool(name="blocks", bufs=blocks) as block_pool,
+        tc.tile_pool(name="pieces", bufs=4) as piece_pool,
+    ):
+        offsets = held.tile([PARTITIONS, entries // OFFSETS_PER_COLUMN], U16, name="offsets")
+        nc.sync.dma_start(offsets[:], offs)
+
+        tables, streams = [], []
+        for b in range(blocks):
+            block_rows = slice(b * PARTITIONS, (b + 1) * PARTITIONS)
+            table = block_pool.tile([PARTITIONS, columns], BF16, name="table")
+            nc.sync.dma_start(table[:], tab[block_rows, :])
+            stream = block_pool.tile([PARTITIONS, entries], F32, name="stream")
+            nc.sync.dma_start(stream[:], y[block_rows, :])
+            tables.append(table)
+            streams.append(stream)
+
+        for b in range(blocks):
+            block_rows = slice(b * PARTITIONS, (b + 1) * PARTITIONS)
+            for p in range(pieces):
+                cols = slice(p * PIECE, (p + 1) * PIECE)
+                piece_offsets = offsets[:, p * piece_columns : (p + 1) * piece_columns]
+                gate = piece_pool.tile([PARTITIONS, PIECE], F32, name="gate")
+                nc.scalar.activation(gate[:], tables[b][:].indirect(piece_offsets), SILU)
+                product = piece_pool.tile([PARTITIONS, PIECE], F32, name="product")
+                nc.vector.tensor_tensor(product[:], gate[:], streams[b][:, cols], MULT)
+                nc.sync.dma_start(out[block_rows, cols], product[:])

@@ -25,6 +25,11 @@ def tile_lookup_gate_silu_out_kernel(tc, tab, y, offs, out):
         offsets = held.tile([PARTITIONS, entries // OFFSETS_PER_COLUMN], U16, name="offsets")
         nc.sync.dma_start(offsets[:], offs)
 
+        zeros = held.tile([PARTITIONS, 1], F32, name="zeros")
+        nc.vector.memset(zeros[:], 0.0)
+        warm = held.tile([PARTITIONS, 1], F32, name="warm")
+        nc.scalar.activation(warm[:], zeros[:], SILU)
+
         tables, streams = [], []
         for b in range(blocks):
             block_rows = slice(b * PARTITIONS, (b + 1) * PARTITIONS)

@@ -6,7 +6,20 @@ MULT = mybir.AluOpType.mult
 
 PARTITIONS = 128
 OFFSETS_PER_COLUMN = 16
-PIECE = 512
+FIRST_PIECE = 512
+SHORTEST_PIECE = 128
+
+
+def list_pieces(entries, last_block):
+    length = FIRST_PIECE
+    pieces = [(first, length) for first in range(0, entries - length, length)]
+    first = entries - length
+    while last_block and length > SHORTEST_PIECE:
+        length = length // 2
+        pieces.append((first, length))
+        first = first + length
+    pieces.append((first, length))
+    return pieces
 
 
 def tile_lookup_gate_silu_out_kernel(tc, tab, y, offs, out):
@@ -14,13 +27,10 @@ def tile_lookup_gate_silu_out_kernel(tc, tab, y, offs, out):
     rows, columns = tab.shape
     entries = y.shape[1]
     blocks = rows // PARTITIONS
-    pieces = entries // PIECE
-    piece_columns = PIECE // OFFSETS_PER_COLUMN
 
     with (
         tc.tile_pool(name="held", bufs=1) as held,
         tc.tile_pool(name="blocks", bufs=blocks) as block_pool,
-        tc.tile_pool(name="pieces", bufs=4) as piece_pool,
     ):
         offsets = held.tile([PARTITIONS, entries // OFFSETS_PER_COLUMN], U16, name="offsets")
         nc.sync.dma_start(offsets[:], offs)
@@ -42,11 +52,11 @@ def tile_lookup_gate_silu_out_kernel(tc, tab, y, offs, out):
 
         for b in range(blocks):
             block_rows = slice(b * PARTITIONS, (b + 1) * PARTITIONS)
-            for p in range(pieces):
-                cols = slice(p * PIECE, (p + 1) * PIECE)
-                piece_offsets = offsets[:, p * piece_columns : (p + 1) * piece_columns]
-                gate = piece_pool.tile([PARTITIONS, PIECE], F32, name="gate")
-                nc.scalar.activation(gate[:], tables[b][:].indirect(piece_offsets), SILU)
-                product = piece_pool.tile([PARTITIONS, PIECE], F32, name="product")
-                nc.vector.tensor_tensor(product[:], gate[:], streams[b][:, cols], MULT)
-                nc.sync.dma_start(out[block_rows, cols], product[:])
+            gate = block_pool.tile([PARTITIONS, entries], F32, name="gate")
+            product = block_pool.tile([PARTITIONS, entries], F32, name="product")
+            for first, length in list_pieces(entries, last_block=b == blocks - 1):
+                cols = slice(first, first + length)
+                piece_offsets = offsets[:, first // OFFSETS_PER_COLUMN : (first + length) // OFFSETS_PER_COLUMN]
+                nc.scalar.activation(gate[:, cols], tables[b][:].indirect(piece_offsets), SILU)
+                nc.vector.tensor_tensor(product[:, cols], gate[:, cols], streams[b][:, cols], MULT)
+                nc.sync.dma_start(out[block_rows, cols], product[:, cols])

import concourse.mybir as mybir

BF16, F32, U16 = mybir.dt.bfloat16, mybir.dt.float32, mybir.dt.uint16
SILU = mybir.ActivationFunctionType.Silu
MULT = mybir.AluOpType.mult

PARTITIONS = 128
OFFSETS_PER_COLUMN = 16
FIRST_PIECE = 512
SHORTEST_PIECE = 128


def list_pieces(entries, last_block):
    length = FIRST_PIECE
    pieces = [(first, length) for first in range(0, entries - length, length)]
    first = entries - length
    while last_block and length > SHORTEST_PIECE:
        length = length // 2
        pieces.append((first, length))
        first = first + length
    pieces.append((first, length))
    return pieces


def tile_lookup_gate_silu_out_kernel(tc, tab, y, offs, out):
    nc = tc.nc
    rows, columns = tab.shape
    entries = y.shape[1]
    blocks = rows // PARTITIONS

    with (
        tc.tile_pool(name="held", bufs=1) as held,
        tc.tile_pool(name="blocks", bufs=blocks) as block_pool,
    ):
        offsets = held.tile([PARTITIONS, entries // OFFSETS_PER_COLUMN], U16, name="offsets")
        nc.sync.dma_start(offsets[:], offs)

        zeros = held.tile([PARTITIONS, 1], F32, name="zeros")
        nc.vector.memset(zeros[:], 0.0)
        warm = held.tile([PARTITIONS, 1], F32, name="warm")
        nc.scalar.activation(warm[:], zeros[:], SILU)

        tables, streams = [], []
        for b in range(blocks):
            block_rows = slice(b * PARTITIONS, (b + 1) * PARTITIONS)
            table = block_pool.tile([PARTITIONS, columns], BF16, name="table")
            nc.sync.dma_start(table[:], tab[block_rows, :])
            stream = block_pool.tile([PARTITIONS, entries], F32, name="stream")
            nc.sync.dma_start(stream[:], y[block_rows, :])
            tables.append(table)
            streams.append(stream)

        for b in range(blocks):
            block_rows = slice(b * PARTITIONS, (b + 1) * PARTITIONS)
            gate = block_pool.tile([PARTITIONS, entries], F32, name="gate")
            product = block_pool.tile([PARTITIONS, entries], F32, name="product")
            for first, length in list_pieces(entries, last_block=b == blocks - 1):
                cols = slice(first, first + length)
                piece_offsets = offsets[:, first // OFFSETS_PER_COLUMN : (first + length) // OFFSETS_PER_COLUMN]
                nc.scalar.activation(gate[:, cols], tables[b][:].indirect(piece_offsets), SILU)
                nc.vector.tensor_tensor(product[:, cols], gate[:, cols], streams[b][:, cols], MULT)
                nc.sync.dma_start(out[block_rows, cols], product[:, cols])
